import numpy as np
import ml_dtypes


def mxq(x, axis, fmt="e4m3"):
    dtype, down = {"e4m3": (ml_dtypes.float8_e4m3fn, 7), "e5m2": (ml_dtypes.float8_e5m2, 14)}[fmt]
    v = np.moveaxis(np.asarray(x, np.float32).astype(ml_dtypes.bfloat16).astype(np.float64), axis, -1)
    blocks = v.reshape(v.shape[:-1] + (-1, 32))
    amax = np.abs(blocks).max(-1, keepdims=True)
    byte = np.maximum(np.where(amax > 0, np.frexp(amax)[1] - 1 + 127, 0) - down, 1)
    scale = np.exp2(byte - 127.0)
    codes = (blocks / scale).astype(np.float32).astype(dtype).astype(np.float64)
    return np.moveaxis((codes * scale).reshape(v.shape), -1, axis)


WIDE = False


def mx_kscale(k):
    if not WIDE:
        return np.ones(k)
    levels = np.array([10, -10, 5, -5, 0])
    if k % 512:
        return np.exp2(np.random.permutation(np.resize(levels, k // 32))).repeat(32)
    a = np.empty((k // 512, 16))
    for p in range(k // 512):
        a[p, :8] = np.random.permutation(np.resize(levels, 8))
        for g in range(8):
            far = levels[np.abs(levels - a[p, g]) >= 10]
            a[p, g + 8] = far[np.random.randint(len(far))]
    return np.exp2(a.ravel()).repeat(32)


BF16 = ml_dtypes.bfloat16


def bf(x):
    return np.asarray(x, np.float32).astype(BF16)


def f64(x):
    return np.asarray(x).astype(np.float64)


E2M1 = np.array([0.0, 0.5, 1.0, 1.5, 2.0, 3.0, 4.0, 6.0, -0.0, -0.5, -1.0, -1.5, -2.0, -3.0, -4.0, -6.0])


def pack_weight(w, fmt):
    k, n = w.shape
    w = f64(bf(w)).reshape(k // 32, 32, n)
    amax = np.abs(w).max(1)
    if fmt == "e4m3":
        byte = np.frexp(amax)[1] - 1 + 127 - 7
    else:
        mant, ex = np.frexp(amax / 6.0)
        byte = np.where(mant > 0.5, ex, ex - 1) + 127
    byte = np.clip(np.where(amax > 0, byte, 1), 1, 254)
    scaled = (w * np.exp2(127.0 - byte)[:, None, :]).reshape(k, n).astype(np.float32)
    by_word = np.ascontiguousarray(scaled.reshape(k // 512, 128, 4, n).transpose(0, 1, 3, 2))
    if fmt == "e4m3":
        words = by_word.astype(ml_dtypes.float8_e4m3fn).view(np.uint8)
    else:
        c = by_word.astype(ml_dtypes.float4_e2m1fn).view(np.uint8) & 0xF
        words = c[..., 0::2] | (c[..., 1::2] << 4)
    return np.ascontiguousarray(words), np.ascontiguousarray(byte.astype(np.uint8).reshape(k // 512, 16, n))


def unpack_weight(words, scales, fmt):
    g, p, n, _ = words.shape
    if fmt == "e4m3":
        vals = np.ascontiguousarray(words).view(ml_dtypes.float8_e4m3fn).astype(np.float64)
    else:
        nib = np.empty((g, p, n, 4), np.uint8)
        nib[..., 0::2] = words & 0xF
        nib[..., 1::2] = words >> 4
        vals = E2M1[nib]
    vals = vals * np.repeat(np.exp2(scales.astype(np.float64) - 127.0), 8, axis=1)[..., None]
    return vals.transpose(0, 1, 3, 2).reshape(g * 512, n)
def pack4(w):
    words, scales = pack_weight(w, "e2m1")
    return words.reshape(words.shape[0], 128, -1), scales


def unpack4(words, scales):
    return unpack_weight(words.reshape(words.shape[0], 128, -1, 2), scales, "e2m1")


G, U, F, I = 4, 768, 512, 1024
ALPHA, SEEN, RIDGE = 3.0, 0.25, 0.5


def setup_inputs():
    s = mx_kscale(G * F).reshape(G, F)
    t = mx_kscale(G * I).reshape(G, I)
    y = np.random.standard_normal((G, I, F)) / np.sqrt(F)
    seen = np.random.random((G, U, I)) < SEEN
    count = 2.0 * np.random.random((G, U, I)) * seen
    yt_words, yt_scales = pack4((y.transpose(0, 2, 1) / s[:, :, None]).reshape(G * F, I))
    y_words, y_scales = pack4((y / t[:, :, None]).reshape(G * I, F))
    return {"x": bf(0.5 * np.random.standard_normal((G, U, F)) * s[:, None, :]),
            "yt_words": yt_words, "yt_scales": yt_scales,
            "pref": bf(seen * 1.0),
            "conf": bf((1.0 + ALPHA * count) * t[:, None, :]),
            "y_words": y_words, "y_scales": y_scales,
            "ridge": bf(RIDGE * (1.0 + np.random.random((G, F))) / s)}


def reference(x, yt_words, yt_scales, pref, conf, y_words, y_scales, ridge):
    x = f64(x)
    yt = unpack4(yt_words, yt_scales).reshape(G, F, I)
    y = unpack4(y_words, y_scales).reshape(G, I, F)
    score = mxq(x, 2, "e4m3") @ yt
    e = f64(conf) * (score - f64(pref))
    grad = mxq(e, 2, "e4m3") @ y
    return grad + f64(ridge)[:, None, :] * x

@@ -1,0 +1,332 @@
+from contextlib import ExitStack
+
+import concourse.mybir as mybir
+from concourse.masks import make_identity
+
+MARKETS, USERS, FACTORS, ITEMS = 4, 768, 512, 1024
+FLOPS = 2 * 2 * MARKETS * USERS * FACTORS * ITEMS
+
+F32 = mybir.dt.float32
+BF16 = mybir.dt.bfloat16
+I32 = mybir.dt.int32
+U32 = mybir.dt.uint32
+U8 = mybir.dt.uint8
+FP8X4 = mybir.dt.float8_e4m3fn_x4
+FP4X4 = mybir.dt.float4_e2m1fn_x4
+ALU = mybir.AluOpType
+ACT = mybir.ActivationFunctionType
+
+P = 128
+PACK = 4
+K_PASS = P * PACK
+BANK = 512
+BANKS = 8
+ITEM_PASSES = ITEMS // K_PASS
+MAX_ROWS = 2
+LOAD_AHEAD = 6
+POOL_COLS_PER_BANK = 256
+POOL_COLS_LESS = 128
+POOL_FROM = 2
+
+STEP_ROWS = [[2, 2, 2], [2, 2, 2], [2, 2, 2], [2, 2, 2]]
+
+
+def tile_implicit_als_gradient_s14_kernel(tc, x, yt_words, yt_scales, pref, conf, y_words, y_scales, ridge, out):
+    nc = tc.nc
+
+    steps = []
+    for market in range(MARKETS):
+        first = 0
+        for rows in STEP_ROWS[market]:
+            steps.append((market, first, rows))
+            first = first + rows * P
+    n_steps = len(steps)
+
+    def users_of(ap, s):
+        market, first, rows = steps[s]
+        return ap[market, first : first + rows * P, :].rearrange("(p r) c -> p r c", r=rows)
+
+    with ExitStack() as ctx:
+        keep = ctx.enter_context(tc.tile_pool(name="keep", bufs=1))
+        work = ctx.enter_context(tc.tile_pool(name="work", bufs=1))
+        psum = ctx.enter_context(tc.psum_pool(name="psum", bufs=1))
+        ctx.enter_context(tc.manual_schedule())
+
+        taken = []
+
+        def next_bank():
+            n = len(taken)
+            bank = psum.tile([P, BANK], F32, name="bank%d" % n, tag="bank%d" % (n % BANKS))
+            taken.append(n)
+            return bank
+
+        def ring(kind, s, depth, shape, dtype):
+            return work.tile(shape, dtype, name="%s%d" % (kind, s), tag="%s%d" % (kind, s % depth), align_bytes=64)
+
+        ident = keep.tile([P, P], F32)
+        yt_plane = keep.tile([P, MARKETS, ITEMS], U8, align_bytes=64)
+        y_plane = keep.tile([P, MARKETS * ITEM_PASSES, FACTORS], U8, align_bytes=64)
+        ridge_bf = keep.tile([P, MARKETS, PACK], BF16)
+        ridge_col = keep.tile([P, MARKETS, PACK], F32)
+
+        nc.vector.memset(yt_plane[:].rearrange("p m n -> p (m n)").bitcast(I32), 0)
+        nc.vector.memset(y_plane[:].rearrange("p m n -> p (m n)").bitcast(I32), 0)
+        make_identity(nc, ident[:])
+
+        x_sb, pref_sb, conf_sb, yt_sb, y_sb = {}, {}, {}, {}, {}
+        x_grouped, x_codes, x_plane = {}, {}, {}
+        x_bank, score_bank, e_bank, grad_bank, rx_bank = {}, {}, {}, {}, {}
+        resid, e_sb, e_grouped, e_codes, e_plane, rx_t, result = {}, {}, {}, {}, {}, {}, {}
+
+        def load_plane(plane, scales, passes):
+            for q in range(4):
+                nc.sync.dma_start(
+                    out=plane[32 * q : 32 * q + 4, passes, :].bitcast(I32),
+                    in_=scales[passes, 4 * q : 4 * q + 4, :].rearrange("g r n -> r g n").bitcast(I32),
+                )
+
+        def load_x(s):
+            rows = steps[s][2]
+            x_sb[s] = keep.tile([P, rows, FACTORS], BF16, name="x%d" % s)
+            nc.sync.dma_start(out=x_sb[s][:], in_=users_of(x, s))
+
+        def load_yt(market):
+            yt_sb[market] = keep.tile([P, 2 * ITEMS], U8, name="yt%d" % market, align_bytes=64)
+            nc.sync.dma_start(out=yt_sb[market][:].bitcast(I32), in_=yt_words[market].bitcast(I32))
+
+        def load_y(market):
+            y_sb[market] = keep.tile([P, ITEM_PASSES, 2 * FACTORS], U8, name="y%d" % market, align_bytes=64)
+            passes = y_words[ITEM_PASSES * market : ITEM_PASSES * (market + 1)]
+            nc.sync.dma_start(out=y_sb[market][:].bitcast(I32), in_=passes.rearrange("g p n -> p g n").bitcast(I32))
+
+        def load_pref(s):
+            rows = steps[s][2]
+            pref_sb[s] = keep.tile([P, rows, ITEMS], BF16, name="pref%d" % s)
+            nc.sync.dma_start(out=pref_sb[s][:], in_=users_of(pref, s))
+
+        def load_conf(s):
+            rows = steps[s][2]
+            conf_sb[s] = keep.tile([P, rows, ITEMS], BF16, name="conf%d" % s)
+            nc.sync.dma_start(out=conf_sb[s][:], in_=users_of(conf, s))
+
+        def load_for(k):
+            if live(k + 1) and steps[k + 1][1] == 0:
+                load_yt(steps[k + 1][0])
+            if live(k + 2):
+                load_x(k + 2)
+            if live(k):
+                load_pref(k)
+            if live(k - 1):
+                load_conf(k - 1)
+            if live(k - 3) and steps[k - 3][1] == 0:
+                load_y(steps[k - 3][0])
+
+        def transpose_x(s):
+            rows = steps[s][2]
+            words = x_sb[s][:].bitcast(F32)
+            x_bank[s] = next_bank()
+            for h in range(2):
+                for r in range(rows):
+                    c = (h * rows + r) * P
+                    nc.tensor.transpose(x_bank[s][:, c : c + P], words[:, r, h : 2 * P : 2], ident[:])
+
+        def group_x(s):
+            rows = steps[s][2]
+            x_grouped[s] = ring("xg", s, 4, [P, rows * P * PACK], BF16)
+            nc.scalar.copy(
+                out=x_grouped[s][:].bitcast(F32).rearrange("p (c h) -> p c h", h=2),
+                in_=x_bank[s][:, : 2 * rows * P].rearrange("p (h c) -> p c h", h=2),
+            )
+
+        def quantize_x(s):
+            rows = steps[s][2]
+            x_codes[s] = ring("xc", s, 3, [P, rows * P], U32)
+            x_plane[s] = ring("xs", s, 3, [P, rows * P], U8)
+            nc.vector.quantize_mx(out=x_codes[s][:].bitcast(FP8X4), scales=x_plane[s][:], in_=x_grouped[s][:])
+
+        def scale_x(s):
+            market, first, rows = steps[s]
+            rx_t[s] = ring("rxt", s, 2, [P, PACK, rows * P], F32)
+            slots = x_grouped[s][:].rearrange("p (c t) -> p t c", t=PACK)
+            for t in range(PACK):
+                nc.scalar.activation(out=rx_t[s][:, t, :], in_=slots[:, t, :], func=ACT.Copy, scale=ridge_col[:, market, t : t + 1])
+
+        def transpose_rx(s):
+            for r in range(steps[s][2]):
+                rx_bank[s, r] = next_bank()
+                for t in range(PACK):
+                    nc.tensor.transpose(rx_bank[s, r][:, t * P : (t + 1) * P], rx_t[s][:, t, r * P : (r + 1) * P], ident[:])
+
+        def copy_rx(s):
+            rows = steps[s][2]
+            result[s] = ring("res", s, 6, [P, rows, FACTORS], F32)
+            for r in range(rows):
+                nc.scalar.copy(
+                    out=result[s][:, r, :].rearrange("u (p t) -> u p t", t=PACK),
+                    in_=rx_bank[s, r][:].rearrange("u (t p) -> u p t", t=PACK),
+                )
+
+        def scores(s):
+            market, first, rows = steps[s]
+            for r in range(rows):
+                for n in range(ITEMS // BANK):
+                    score_bank[s, r, n] = next_bank()
+                    nc.tensor.matmul_mx(
+                        out=score_bank[s, r, n][:],
+                        lhsT=x_codes[s][:, r * P : (r + 1) * P].bitcast(FP8X4),
+                        lhsT_scale=x_plane[s][:, r * P : (r + 1) * P],
+                        rhs=yt_sb[market][:, 2 * n * BANK : 2 * (n + 1) * BANK].bitcast(FP4X4),
+                        rhs_scale=yt_plane[:, market, n * BANK : (n + 1) * BANK],
+                        start=True,
+                        stop=True,
+                    )
+
+        def subtract_pref(s):
+            rows = steps[s][2]
+            resid[s] = ring("resid", s, 2, [P, rows * ITEMS], F32)
+            for r in range(rows):
+                for n in range(ITEMS // BANK):
+                    c = r * ITEMS + n * BANK
+                    nc.vector.tensor_tensor(
+                        out=resid[s][:, c : c + BANK],
+                        in0=score_bank[s, r, n][:],
+                        in1=pref_sb[s][:, r, n * BANK : (n + 1) * BANK],
+                        op=ALU.subtract,
+                    )
+
+        def weigh(engine, s, cols):
+            flat = conf_sb[s][:].rearrange("p r c -> p (r c)")
+            engine.tensor_tensor(out=e_sb[s][:, cols], in0=resid[s][:, cols], in1=flat[:, cols], op=ALU.mult)
+
+        def transpose_e(s):
+            words = e_sb[s][:].bitcast(F32)
+            for r in range(steps[s][2]):
+                e_bank[s, r] = next_bank()
+                for g in range(ITEM_PASSES):
+                    for h in range(2):
+                        c = (2 * g + h) * P
+                        w = (r * ITEM_PASSES + g) * 2 * P
+                        nc.tensor.transpose(e_bank[s, r][:, c : c + P], words[:, w + h : w + 2 * P : 2], ident[:])
+
+        def group_e(s):
+            rows = steps[s][2]
+            e_grouped[s] = ring("e", s, 2, [P, rows * ITEMS], BF16)
+            words = e_grouped[s][:].bitcast(F32)
+            for r in range(rows):
+                nc.scalar.copy(
+                    out=words[:, r * BANK : (r + 1) * BANK].rearrange("p (g u h) -> p g u h", g=ITEM_PASSES, h=2),
+                    in_=e_bank[s, r][:].rearrange("p (g h u) -> p g u h", g=ITEM_PASSES, h=2),
+                )
+
+        def quantize_e(s):
+            rows = steps[s][2]
+            e_codes[s] = ring("ec", s, 2, [P, rows * ITEM_PASSES * P], U32)
+            e_plane[s] = ring("es", s, 2, [P, rows * ITEM_PASSES * P], U8)
+            nc.vector.quantize_mx(out=e_codes[s][:].bitcast(FP8X4), scales=e_plane[s][:], in_=e_grouped[s][:])
+
+        def gradient(s):
+            market, first, rows = steps[s]
+            for r in range(rows):
+                grad_bank[s, r] = next_bank()
+                for g in range(ITEM_PASSES):
+                    c = (r * ITEM_PASSES + g) * P
+                    nc.tensor.matmul_mx(
+                        out=grad_bank[s, r][:],
+                        lhsT=e_codes[s][:, c : c + P].bitcast(FP8X4),
+                        lhsT_scale=e_plane[s][:, c : c + P],
+                        rhs=y_sb[market][:, g, :].bitcast(FP4X4),
+                        rhs_scale=y_plane[:, market * ITEM_PASSES + g, :],
+                        start=(g == 0),
+                        stop=(g == ITEM_PASSES - 1),
+                    )
+
+        def finish(s):
+            last = s == n_steps - 1
+            for r in range(steps[s][2]):
+                nc.vector.tensor_tensor(out=result[s][:, r, :], in0=grad_bank[s, r][:], in1=result[s][:, r, :], op=ALU.add)
+                if last:
+                    nc.sync.dma_start(out=users_of(out, s)[:, r, :], in_=result[s][:, r, :])
+            if not last:
+                nc.sync.dma_start(out=users_of(out, s), in_=result[s][:])
+
+        def live(s):
+            return 0 <= s < n_steps
+
+        load_x(0)
+        load_yt(0)
+        load_plane(yt_plane, yt_scales, slice(0, 1))
+        load_pref(0)
+        load_x(1)
+        load_x(2)
+        load_pref(1)
+        load_conf(0)
+        nc.sync.dma_start(out=ridge_bf[:], in_=ridge.rearrange("m (p t) -> p m t", t=PACK))
+        load_x(3)
+        load_for(2)
+        load_plane(yt_plane, yt_scales, slice(1, MARKETS))
+        load_plane(y_plane, y_scales, slice(0, MARKETS * ITEM_PASSES))
+        for k in range(3, LOAD_AHEAD):
+            load_for(k)
+
+        transpose_x(0)
+        group_x(0)
+        quantize_x(0)
+        scores(0)
+        transpose_x(1)
+        group_x(1)
+        subtract_pref(0)
+        quantize_x(1)
+        nc.scalar.copy(out=ridge_col[:], in_=ridge_bf[:])
+
+        for k in range(n_steps):
+            load_for(k + LOAD_AHEAD)
+            if live(k - 3):
+                gradient(k - 3)
+            banks_read = (2 * steps[k][2] if live(k) else 0) + (steps[k - 3][2] if live(k - 3) else 0)
+            if live(k - 1):
+                width = steps[k - 1][2] * ITEMS
+                split = min(width, max(0, banks_read * POOL_COLS_PER_BANK - POOL_COLS_LESS)) if k - 1 >= POOL_FROM else 0
+                e_sb[k - 1] = ring("e", k - 1, 2, [P, width], BF16)
+                if split > 0:
+                    weigh(nc.gpsimd, k - 1, slice(0, split))
+            if k > 0:
+                subtract_pref(k)
+            if live(k - 3):
+                finish(k - 3)
+            if live(k + 2):
+                transpose_x(k + 2)
+                group_x(k + 2)
+            if live(k - 2):
+                transpose_e(k - 2)
+                group_e(k - 2)
+            if live(k - 1):
+                transpose_rx(k - 1)
+                copy_rx(k - 1)
+            scale_x(k)
+            if live(k - 1) and split < width:
+                weigh(nc.vector, k - 1, slice(split, width))
+            if live(k + 2):
+                quantize_x(k + 2)
+            if live(k - 2):
+                quantize_e(k - 2)
+            if live(k + 1):
+                scores(k + 1)
+
+        a, b, c = n_steps - 3, n_steps - 2, n_steps - 1
+        transpose_e(b)
+        group_e(b)
+        gradient(a)
+        transpose_rx(c)
+        copy_rx(c)
+        width = steps[c][2] * ITEMS
+        e_sb[c] = ring("e", c, 2, [P, width], BF16)
+        weigh(nc.vector, c, slice(0, width))
+        quantize_e(b)
+        finish(a)
+        transpose_e(c)
+        group_e(c)
+        gradient(b)
+        quantize_e(c)
+        finish(b)
+        gradient(c)
+        finish(c)

@@ -25,8 +25,10 @@ ITEM_PASSES = ITEMS // K_PASS
 MAX_ROWS = 2
 LOAD_AHEAD = 6
 POOL_COLS_PER_BANK = 256
-POOL_COLS_LESS = 128
-POOL_FROM = 2
+POOL_COLS_LESS = 256
+HEAD0 = 3
+LATE_PLANES = 4
+WARM = [0, 0, 0, 0]
 
 STEP_ROWS = [[2, 2, 2], [2, 2, 2], [2, 2, 2], [2, 2, 2]]
 
@@ -110,16 +112,16 @@ def tile_implicit_als_gradient_s14_kernel(tc, x, yt_words, yt_scales, pref, conf
             nc.sync.dma_start(out=conf_sb[s][:], in_=users_of(conf, s))
 
         def load_for(k):
-            if live(k + 1) and steps[k + 1][1] == 0:
-                load_yt(steps[k + 1][0])
-            if live(k + 2):
-                load_x(k + 2)
             if live(k):
                 load_pref(k)
             if live(k - 1):
                 load_conf(k - 1)
             if live(k - 3) and steps[k - 3][1] == 0:
                 load_y(steps[k - 3][0])
+            if live(k + 2):
+                load_x(k + 2)
+            if live(k + 1) and steps[k + 1][1] == 0:
+                load_yt(steps[k + 1][0])
 
         def transpose_x(s):
             rows = steps[s][2]
@@ -181,32 +183,38 @@ def tile_implicit_als_gradient_s14_kernel(tc, x, yt_words, yt_scales, pref, conf
                         stop=True,
                     )
 
-        def subtract_pref(s):
+        def subtract_pref(s, banks):
             rows = steps[s][2]
-            resid[s] = ring("resid", s, 2, [P, rows * ITEMS], F32)
-            for r in range(rows):
-                for n in range(ITEMS // BANK):
-                    c = r * ITEMS + n * BANK
+            if s not in resid:
+                resid[s] = ring("resid", s, 2, [P, rows * ITEMS], F32)
+            for b in banks:
+                for r, n in [divmod(b, ITEM_PASSES)]:
+                    q = (r * ITEM_PASSES + n) * P
                     nc.vector.tensor_tensor(
-                        out=resid[s][:, c : c + BANK],
-                        in0=score_bank[s, r, n][:],
-                        in1=pref_sb[s][:, r, n * BANK : (n + 1) * BANK],
+                        out=resid[s][:].rearrange("u (h q e) -> u h q e", h=2, e=2)[:, :, q : q + P, :],
+                        in0=score_bank[s, r, n][:].rearrange("u (q h e) -> u h q e", h=2, e=2),
+                        in1=pref_sb[s][:, r, n * BANK : (n + 1) * BANK].rearrange("u (q h e) -> u h q e", h=2, e=2),
                         op=ALU.subtract,
                     )
 
         def weigh(engine, s, cols):
-            flat = conf_sb[s][:].rearrange("p r c -> p (r c)")
-            engine.tensor_tensor(out=e_sb[s][:, cols], in0=resid[s][:, cols], in1=flat[:, cols], op=ALU.mult)
+            quads = slice(cols.start // PACK, cols.stop // PACK)
+            engine.tensor_tensor(
+                out=e_sb[s][:].rearrange("u (h q e) -> u h q e", h=2, e=2)[:, :, quads, :],
+                in0=resid[s][:].rearrange("u (h q e) -> u h q e", h=2, e=2)[:, :, quads, :],
+                in1=conf_sb[s][:].rearrange("u r (q h e) -> u h (r q) e", h=2, e=2)[:, :, quads, :],
+                op=ALU.mult,
+            )
 
         def transpose_e(s):
-            words = e_sb[s][:].bitcast(F32)
+            words = e_sb[s][:].bitcast(F32).rearrange("u (h q) -> u h q", h=2)
             for r in range(steps[s][2]):
                 e_bank[s, r] = next_bank()
                 for g in range(ITEM_PASSES):
                     for h in range(2):
                         c = (2 * g + h) * P
-                        w = (r * ITEM_PASSES + g) * 2 * P
-                        nc.tensor.transpose(e_bank[s, r][:, c : c + P], words[:, w + h : w + 2 * P : 2], ident[:])
+                        q = (r * ITEM_PASSES + g) * P
+                        nc.tensor.transpose(e_bank[s, r][:, c : c + P], words[:, h, q : q + P], ident[:])
 
         def group_e(s):
             rows = steps[s][2]
@@ -252,80 +260,115 @@ def tile_implicit_als_gradient_s14_kernel(tc, x, yt_words, yt_scales, pref, conf
         def live(s):
             return 0 <= s < n_steps
 
+        def pool_share(s, banks_read):
+            width = steps[s][2] * ITEMS
+            share = min(width, max(0, banks_read * POOL_COLS_PER_BANK - POOL_COLS_LESS))
+            e_sb[s] = ring("e", s, 2, [P, width], BF16)
+            if share > 0:
+                weigh(nc.gpsimd, s, slice(width - share, width))
+            return slice(0, width - share)
+
+        def warm(passes):
+            s = n_steps - 1
+            for n in range(passes):
+                bank = next_bank()
+                nc.tensor.matmul_mx(
+                    out=bank[:],
+                    lhsT=x_codes[s][:, :P].bitcast(FP8X4),
+                    lhsT_scale=x_plane[s][:, :P],
+                    rhs=yt_sb[MARKETS - 1][:, : 2 * BANK].bitcast(FP4X4),
+                    rhs_scale=yt_plane[:, MARKETS - 1, :BANK],
+                    start=True,
+                    stop=True,
+                )
+
         load_x(0)
+        load_x(1)
         load_yt(0)
         load_plane(yt_plane, yt_scales, slice(0, 1))
         load_pref(0)
-        load_x(1)
         load_x(2)
         load_pref(1)
         load_conf(0)
         nc.sync.dma_start(out=ridge_bf[:], in_=ridge.rearrange("m (p t) -> p m t", t=PACK))
         load_x(3)
         load_for(2)
-        load_plane(yt_plane, yt_scales, slice(1, MARKETS))
-        load_plane(y_plane, y_scales, slice(0, MARKETS * ITEM_PASSES))
-        for k in range(3, LOAD_AHEAD):
+        load_plane(yt_plane, yt_scales, slice(1, 2))
+        load_plane(y_plane, y_scales, slice(0, ITEM_PASSES))
+        for k in range(3, LOAD_AHEAD + 2):
             load_for(k)
+            if k == LATE_PLANES:
+                load_plane(yt_plane, yt_scales, slice(2, MARKETS))
+                load_plane(y_plane, y_scales, slice(ITEM_PASSES, MARKETS * ITEM_PASSES))
 
         transpose_x(0)
         group_x(0)
         quantize_x(0)
-        scores(0)
         transpose_x(1)
         group_x(1)
-        subtract_pref(0)
         quantize_x(1)
+        scores(0)
+        transpose_x(2)
+        group_x(2)
+        subtract_pref(0, [0, 1, 2])
+        scores(1)
+        quantize_x(2)
+        subtract_pref(0, [3])
         nc.scalar.copy(out=ridge_col[:], in_=ridge_bf[:])
+        scale_x(0)
+        rest = pool_share(0, HEAD0)
+        subtract_pref(1, [0, 1, 2])
+        transpose_x(3)
+        group_x(3)
+        scale_x(1)
+        scores(2)
+        weigh(nc.vector, 0, rest)
+        quantize_x(3)
+        subtract_pref(1, [3])
+        transpose_rx(0)
+        copy_rx(0)
 
-        for k in range(n_steps):
+        for k in range(2, n_steps):
             load_for(k + LOAD_AHEAD)
             if live(k - 3):
                 gradient(k - 3)
-            banks_read = (2 * steps[k][2] if live(k) else 0) + (steps[k - 3][2] if live(k - 3) else 0)
-            if live(k - 1):
-                width = steps[k - 1][2] * ITEMS
-                split = min(width, max(0, banks_read * POOL_COLS_PER_BANK - POOL_COLS_LESS)) if k - 1 >= POOL_FROM else 0
-                e_sb[k - 1] = ring("e", k - 1, 2, [P, width], BF16)
-                if split > 0:
-                    weigh(nc.gpsimd, k - 1, slice(0, split))
-            if k > 0:
-                subtract_pref(k)
+            rest = pool_share(k - 1, 2 * steps[k][2] + (steps[k - 3][2] if live(k - 3) else 0))
+            subtract_pref(k, range(2 * steps[k][2]))
             if live(k - 3):
                 finish(k - 3)
             if live(k + 2):
                 transpose_x(k + 2)
                 group_x(k + 2)
-            if live(k - 2):
-                transpose_e(k - 2)
-                group_e(k - 2)
-            if live(k - 1):
-                transpose_rx(k - 1)
-                copy_rx(k - 1)
+            transpose_e(k - 2)
+            group_e(k - 2)
             scale_x(k)
-            if live(k - 1) and split < width:
-                weigh(nc.vector, k - 1, slice(split, width))
+            weigh(nc.vector, k - 1, rest)
             if live(k + 2):
                 quantize_x(k + 2)
-            if live(k - 2):
-                quantize_e(k - 2)
+            quantize_e(k - 2)
             if live(k + 1):
                 scores(k + 1)
+            else:
+                warm(WARM[0])
+            transpose_rx(k - 1)
+            copy_rx(k - 1)
 
         a, b, c = n_steps - 3, n_steps - 2, n_steps - 1
+        warm(WARM[1])
         transpose_e(b)
         group_e(b)
         gradient(a)
         transpose_rx(c)
-        copy_rx(c)
-        width = steps[c][2] * ITEMS
-        e_sb[c] = ring("e", c, 2, [P, width], BF16)
-        weigh(nc.vector, c, slice(0, width))
+        warm(WARM[2])
+        rest = pool_share(c, 0)
+        weigh(nc.vector, c, rest)
         quantize_e(b)
         finish(a)
         transpose_e(c)
         group_e(c)
+        copy_rx(c)
         gradient(b)
+        warm(WARM[3])
         quantize_e(c)
         finish(b)
         gradient(c)

@@ -22,10 +22,10 @@ K_PASS = P * PACK
 BANK = 512
 BANKS = 8
 ITEM_PASSES = ITEMS // K_PASS
-MAX_ROWS = 2
+ROWS = 2
 LOAD_AHEAD = 6
 POOL_COLS_PER_BANK = 256
-POOL_COLS_LESS = 256
+POOL_COLS_LESS = 128
 HEAD0 = 3
 LATE_PLANES = 4
 WARM = [0, 0, 0, 0]
@@ -87,10 +87,11 @@ def tile_implicit_als_gradient_s14_kernel(tc, x, yt_words, yt_scales, pref, conf
                     in_=scales[passes, 4 * q : 4 * q + 4, :].rearrange("g r n -> r g n").bitcast(I32),
                 )
 
-        def load_x(s):
-            rows = steps[s][2]
-            x_sb[s] = keep.tile([P, rows, FACTORS], BF16, name="x%d" % s)
-            nc.sync.dma_start(out=x_sb[s][:], in_=users_of(x, s))
+        def load_x(s, rows=range(ROWS)):
+            tile = keep.tile([P, len(rows), FACTORS], BF16, name="x%d_%d" % (s, rows.start))
+            nc.sync.dma_start(out=tile[:], in_=users_of(x, s)[:, rows.start : rows.stop, :])
+            for r in rows:
+                x_sb[s, r] = tile[:].bitcast(F32)[:, r - rows.start, :]
 
         def load_yt(market):
             yt_sb[market] = keep.tile([P, 2 * ITEMS], U8, name="yt%d" % market, align_bytes=64)
@@ -101,10 +102,11 @@ def tile_implicit_als_gradient_s14_kernel(tc, x, yt_words, yt_scales, pref, conf
             passes = y_words[ITEM_PASSES * market : ITEM_PASSES * (market + 1)]
             nc.sync.dma_start(out=y_sb[market][:].bitcast(I32), in_=passes.rearrange("g p n -> p g n").bitcast(I32))
 
-        def load_pref(s):
-            rows = steps[s][2]
-            pref_sb[s] = keep.tile([P, rows, ITEMS], BF16, name="pref%d" % s)
-            nc.sync.dma_start(out=pref_sb[s][:], in_=users_of(pref, s))
+        def load_pref(s, rows=range(ROWS)):
+            tile = keep.tile([P, len(rows), ITEMS], BF16, name="pref%d_%d" % (s, rows.start))
+            nc.sync.dma_start(out=tile[:], in_=users_of(pref, s)[:, rows.start : rows.stop, :])
+            for r in rows:
+                pref_sb[s, r] = tile[:, r - rows.start, :]
 
         def load_conf(s):
             rows = steps[s][2]
@@ -123,28 +125,31 @@ def tile_implicit_als_gradient_s14_kernel(tc, x, yt_words, yt_scales, pref, conf
             if live(k + 1) and steps[k + 1][1] == 0:
                 load_yt(steps[k + 1][0])
 
-        def transpose_x(s):
-            rows = steps[s][2]
-            words = x_sb[s][:].bitcast(F32)
-            x_bank[s] = next_bank()
+        def transpose_x(s, rows=range(ROWS)):
+            x_bank[s, rows.start] = next_bank()
             for h in range(2):
-                for r in range(rows):
-                    c = (h * rows + r) * P
-                    nc.tensor.transpose(x_bank[s][:, c : c + P], words[:, r, h : 2 * P : 2], ident[:])
+                for r in rows:
+                    c = (h * len(rows) + r - rows.start) * P
+                    nc.tensor.transpose(x_bank[s, rows.start][:, c : c + P], x_sb[s, r][:, h : 2 * P : 2], ident[:])
 
-        def group_x(s):
-            rows = steps[s][2]
-            x_grouped[s] = ring("xg", s, 4, [P, rows * P * PACK], BF16)
+        def group_x(s, rows=range(ROWS)):
+            if s not in x_grouped:
+                x_grouped[s] = ring("xg", s, 4, [P, ROWS * P * PACK], BF16)
             nc.scalar.copy(
-                out=x_grouped[s][:].bitcast(F32).rearrange("p (c h) -> p c h", h=2),
-                in_=x_bank[s][:, : 2 * rows * P].rearrange("p (h c) -> p c h", h=2),
+                out=x_grouped[s][:].bitcast(F32)[:, 2 * P * rows.start : 2 * P * rows.stop].rearrange("p (c h) -> p c h", h=2),
+                in_=x_bank[s, rows.start][:, : 2 * len(rows) * P].rearrange("p (h c) -> p c h", h=2),
             )
 
-        def quantize_x(s):
-            rows = steps[s][2]
-            x_codes[s] = ring("xc", s, 3, [P, rows * P], U32)
-            x_plane[s] = ring("xs", s, 3, [P, rows * P], U8)
-            nc.vector.quantize_mx(out=x_codes[s][:].bitcast(FP8X4), scales=x_plane[s][:], in_=x_grouped[s][:])
+        def quantize_x(s, rows=range(ROWS)):
+            if s not in x_codes:
+                x_codes[s] = ring("xc", s, 3, [P, ROWS * P], U32)
+                x_plane[s] = ring("xs", s, 3, [P, ROWS * P], U8)
+            cols = slice(rows.start * P, rows.stop * P)
+            nc.vector.quantize_mx(
+                out=x_codes[s][:, cols].bitcast(FP8X4),
+                scales=x_plane[s][:, cols],
+                in_=x_grouped[s][:, PACK * cols.start : PACK * cols.stop],
+            )
 
         def scale_x(s):
             market, first, rows = steps[s]
@@ -168,9 +173,9 @@ def tile_implicit_als_gradient_s14_kernel(tc, x, yt_words, yt_scales, pref, conf
                     in_=rx_bank[s, r][:].rearrange("u (t p) -> u p t", t=PACK),
                 )
 
-        def scores(s):
-            market, first, rows = steps[s]
-            for r in range(rows):
+        def scores(s, rows=range(ROWS)):
+            market = steps[s][0]
+            for r in rows:
                 for n in range(ITEMS // BANK):
                     score_bank[s, r, n] = next_bank()
                     nc.tensor.matmul_mx(
@@ -193,7 +198,7 @@ def tile_implicit_als_gradient_s14_kernel(tc, x, yt_words, yt_scales, pref, conf
                     nc.vector.tensor_tensor(
                         out=resid[s][:].rearrange("u (h q e) -> u h q e", h=2, e=2)[:, :, q : q + P, :],
                         in0=score_bank[s, r, n][:].rearrange("u (q h e) -> u h q e", h=2, e=2),
-                        in1=pref_sb[s][:, r, n * BANK : (n + 1) * BANK].rearrange("u (q h e) -> u h q e", h=2, e=2),
+                        in1=pref_sb[s, r][:, n * BANK : (n + 1) * BANK].rearrange("u (q h e) -> u h q e", h=2, e=2),
                         op=ALU.subtract,
                     )
 
@@ -249,7 +254,7 @@ def tile_implicit_als_gradient_s14_kernel(tc, x, yt_words, yt_scales, pref, conf
                     )
 
         def finish(s):
-            last = s == n_steps - 1
+            last = s >= n_steps - 2
             for r in range(steps[s][2]):
                 nc.vector.tensor_tensor(out=result[s][:, r, :], in0=grad_bank[s, r][:], in1=result[s][:, r, :], op=ALU.add)
                 if last:
@@ -282,11 +287,13 @@ def tile_implicit_als_gradient_s14_kernel(tc, x, yt_words, yt_scales, pref, conf
                     stop=True,
                 )
 
-        load_x(0)
-        load_x(1)
+        load_x(0, range(0, 1))
         load_yt(0)
+        load_x(0, range(1, 2))
         load_plane(yt_plane, yt_scales, slice(0, 1))
-        load_pref(0)
+        load_x(1)
+        load_pref(0, range(0, 1))
+        load_pref(0, range(1, 2))
         load_x(2)
         load_pref(1)
         load_conf(0)
@@ -301,30 +308,32 @@ def tile_implicit_als_gradient_s14_kernel(tc, x, yt_words, yt_scales, pref, conf
                 load_plane(yt_plane, yt_scales, slice(2, MARKETS))
                 load_plane(y_plane, y_scales, slice(ITEM_PASSES, MARKETS * ITEM_PASSES))
 
-        transpose_x(0)
-        group_x(0)
-        quantize_x(0)
+        for r in range(ROWS):
+            transpose_x(0, range(r, r + 1))
+            group_x(0, range(r, r + 1))
+            quantize_x(0, range(r, r + 1))
+        scores(0, range(0, 1))
         transpose_x(1)
         group_x(1)
+        scores(0, range(1, 2))
+        subtract_pref(0, [0, 1])
         quantize_x(1)
-        scores(0)
+        scores(1)
+        subtract_pref(0, [2, 3])
         transpose_x(2)
         group_x(2)
-        subtract_pref(0, [0, 1, 2])
-        scores(1)
-        quantize_x(2)
-        subtract_pref(0, [3])
+        transpose_x(3)
+        group_x(3)
         nc.scalar.copy(out=ridge_col[:], in_=ridge_bf[:])
         scale_x(0)
         rest = pool_share(0, HEAD0)
         subtract_pref(1, [0, 1, 2])
-        transpose_x(3)
-        group_x(3)
-        scale_x(1)
+        quantize_x(2)
         scores(2)
         weigh(nc.vector, 0, rest)
         quantize_x(3)
         subtract_pref(1, [3])
+        scale_x(1)
         transpose_rx(0)
         copy_rx(0)
 
@@ -336,29 +345,34 @@ def tile_implicit_als_gradient_s14_kernel(tc, x, yt_words, yt_scales, pref, conf
             subtract_pref(k, range(2 * steps[k][2]))
             if live(k - 3):
                 finish(k - 3)
+            transpose_e(k - 2)
+            group_e(k - 2)
             if live(k + 2):
                 transpose_x(k + 2)
                 group_x(k + 2)
-            transpose_e(k - 2)
-            group_e(k - 2)
-            scale_x(k)
+            if live(k + 1):
+                scale_x(k)
             weigh(nc.vector, k - 1, rest)
+            quantize_e(k - 2)
             if live(k + 2):
                 quantize_x(k + 2)
-            quantize_e(k - 2)
             if live(k + 1):
                 scores(k + 1)
             else:
                 warm(WARM[0])
             transpose_rx(k - 1)
             copy_rx(k - 1)
+            if k == n_steps - 2:
+                scale_x(k + 1)
+            if k == n_steps - 1:
+                transpose_rx(k)
+                copy_rx(k)
 
         a, b, c = n_steps - 3, n_steps - 2, n_steps - 1
         warm(WARM[1])
         transpose_e(b)
         group_e(b)
         gradient(a)
-        transpose_rx(c)
         warm(WARM[2])
         rest = pool_share(c, 0)
         weigh(nc.vector, c, rest)
@@ -366,7 +380,6 @@ def tile_implicit_als_gradient_s14_kernel(tc, x, yt_words, yt_scales, pref, conf
         finish(a)
         transpose_e(c)
         group_e(c)
-        copy_rx(c)
         gradient(b)
         warm(WARM[3])
         quantize_e(c)

@@ -25,7 +25,7 @@ ITEM_PASSES = ITEMS // K_PASS
 ROWS = 2
 LOAD_AHEAD = 6
 POOL_COLS_PER_BANK = 256
-POOL_COLS_LESS = 128
+POOL_COLS_LESS = 288
 HEAD0 = 3
 LATE_PLANES = 4
 WARM = [0, 0, 0, 0]

@@ -18,35 +18,40 @@ ACT = mybir.ActivationFunctionType
 
 P = 128
 PACK = 4
-K_PASS = P * PACK
 BANK = 512
 BANKS = 8
-ITEM_PASSES = ITEMS // K_PASS
+QUADRANTS = 4
+ITEM_PASSES = ITEMS // (P * PACK)
 ROWS = 2
-LOAD_AHEAD = 6
-POOL_COLS_PER_BANK = 256
-POOL_COLS_LESS = 288
-HEAD0 = 3
-LATE_PLANES = 4
-WARM = [0, 0, 0, 0]
+BOTH = range(ROWS)
+STEP_USERS = ROWS * P
+STEPS_PER_MARKET = USERS // STEP_USERS
+STEPS = MARKETS * STEPS_PER_MARKET
+SCORE_BANKS = ROWS * ITEM_PASSES
+E_COLS = ROWS * ITEMS
 
-STEP_ROWS = [[2, 2, 2], [2, 2, 2], [2, 2, 2], [2, 2, 2]]
+POOL_COLS_PER_BANK = 256
+POOL_COLS_LESS = 192
+LOAD_AHEAD = 5
+RESULTS = 8
+LATE_PLANES = 5
 
 
 def tile_implicit_als_gradient_s14_kernel(tc, x, yt_words, yt_scales, pref, conf, y_words, y_scales, ridge, out):
     nc = tc.nc
 
-    steps = []
-    for market in range(MARKETS):
-        first = 0
-        for rows in STEP_ROWS[market]:
-            steps.append((market, first, rows))
-            first = first + rows * P
-    n_steps = len(steps)
+    def live(s):
+        return 0 <= s < STEPS
+
+    def market_of(s):
+        return s // STEPS_PER_MARKET
+
+    def opens_market(s):
+        return live(s) and s % STEPS_PER_MARKET == 0
 
     def users_of(ap, s):
-        market, first, rows = steps[s]
-        return ap[market, first : first + rows * P, :].rearrange("(p r) c -> p r c", r=rows)
+        first = s % STEPS_PER_MARKET * STEP_USERS
+        return ap[market_of(s), first : first + STEP_USERS, :].rearrange("(p r) c -> p r c", r=ROWS)
 
     with ExitStack() as ctx:
         keep = ctx.enter_context(tc.tile_pool(name="keep", bufs=1))
@@ -54,13 +59,12 @@ def tile_implicit_als_gradient_s14_kernel(tc, x, yt_words, yt_scales, pref, conf
         psum = ctx.enter_context(tc.psum_pool(name="psum", bufs=1))
         ctx.enter_context(tc.manual_schedule())
 
-        taken = []
+        banks_taken = []
 
         def next_bank():
-            n = len(taken)
-            bank = psum.tile([P, BANK], F32, name="bank%d" % n, tag="bank%d" % (n % BANKS))
-            taken.append(n)
-            return bank
+            n = len(banks_taken)
+            banks_taken.append(n)
+            return psum.tile([P, BANK], F32, name="bank%d" % n, tag="bank%d" % (n % BANKS))
 
         def ring(kind, s, depth, shape, dtype):
             return work.tile(shape, dtype, name="%s%d" % (kind, s), tag="%s%d" % (kind, s % depth), align_bytes=64)
@@ -75,23 +79,33 @@ def tile_implicit_als_gradient_s14_kernel(tc, x, yt_words, yt_scales, pref, conf
         nc.vector.memset(y_plane[:].rearrange("p m n -> p (m n)").bitcast(I32), 0)
         make_identity(nc, ident[:])
 
-        x_sb, pref_sb, conf_sb, yt_sb, y_sb = {}, {}, {}, {}, {}
-        x_grouped, x_codes, x_plane = {}, {}, {}
-        x_bank, score_bank, e_bank, grad_bank, rx_bank = {}, {}, {}, {}, {}
-        resid, e_sb, e_grouped, e_codes, e_plane, rx_t, result = {}, {}, {}, {}, {}, {}, {}
+        x_pairs, pref_sb, conf_sb, yt_sb, y_sb = {}, {}, {}, {}, {}
+        x_bank, x_grouped, x_codes, x_plane, rx_t, rx_bank, result = {}, {}, {}, {}, {}, {}, {}
+        score_bank, resid, e_sb, e_bank, e_grouped, e_codes, e_plane, grad_bank = {}, {}, {}, {}, {}, {}, {}, {}
+
 
         def load_plane(plane, scales, passes):
-            for q in range(4):
+            for q in range(QUADRANTS):
                 nc.sync.dma_start(
                     out=plane[32 * q : 32 * q + 4, passes, :].bitcast(I32),
                     in_=scales[passes, 4 * q : 4 * q + 4, :].rearrange("g r n -> r g n").bitcast(I32),
                 )
 
-        def load_x(s, rows=range(ROWS)):
+        def load_x(s, rows=BOTH):
             tile = keep.tile([P, len(rows), FACTORS], BF16, name="x%d_%d" % (s, rows.start))
             nc.sync.dma_start(out=tile[:], in_=users_of(x, s)[:, rows.start : rows.stop, :])
             for r in rows:
-                x_sb[s, r] = tile[:].bitcast(F32)[:, r - rows.start, :]
+                x_pairs[s, r] = tile[:].bitcast(F32)[:, r - rows.start, :]
+
+        def load_pref(s, rows=BOTH):
+            tile = keep.tile([P, len(rows), ITEMS], BF16, name="pref%d_%d" % (s, rows.start))
+            nc.sync.dma_start(out=tile[:], in_=users_of(pref, s)[:, rows.start : rows.stop, :])
+            for r in rows:
+                pref_sb[s, r] = tile[:, r - rows.start, :]
+
+        def load_conf(s):
+            conf_sb[s] = keep.tile([P, ROWS, ITEMS], BF16, name="conf%d" % s)
+            nc.sync.dma_start(out=conf_sb[s][:], in_=users_of(conf, s))
 
         def load_yt(market):
             yt_sb[market] = keep.tile([P, 2 * ITEMS], U8, name="yt%d" % market, align_bytes=64)
@@ -102,48 +116,39 @@ def tile_implicit_als_gradient_s14_kernel(tc, x, yt_words, yt_scales, pref, conf
             passes = y_words[ITEM_PASSES * market : ITEM_PASSES * (market + 1)]
             nc.sync.dma_start(out=y_sb[market][:].bitcast(I32), in_=passes.rearrange("g p n -> p g n").bitcast(I32))
 
-        def load_pref(s, rows=range(ROWS)):
-            tile = keep.tile([P, len(rows), ITEMS], BF16, name="pref%d_%d" % (s, rows.start))
-            nc.sync.dma_start(out=tile[:], in_=users_of(pref, s)[:, rows.start : rows.stop, :])
-            for r in rows:
-                pref_sb[s, r] = tile[:, r - rows.start, :]
-
-        def load_conf(s):
-            rows = steps[s][2]
-            conf_sb[s] = keep.tile([P, rows, ITEMS], BF16, name="conf%d" % s)
-            nc.sync.dma_start(out=conf_sb[s][:], in_=users_of(conf, s))
-
         def load_for(k):
             if live(k):
                 load_pref(k)
             if live(k - 1):
                 load_conf(k - 1)
-            if live(k - 3) and steps[k - 3][1] == 0:
-                load_y(steps[k - 3][0])
+            if opens_market(k - 3):
+                load_y(market_of(k - 3))
             if live(k + 2):
                 load_x(k + 2)
-            if live(k + 1) and steps[k + 1][1] == 0:
-                load_yt(steps[k + 1][0])
+            if opens_market(k + 1):
+                load_yt(market_of(k + 1))
 
-        def transpose_x(s, rows=range(ROWS)):
+
+        def transpose_x(s, rows=BOTH):
             x_bank[s, rows.start] = next_bank()
             for h in range(2):
                 for r in rows:
                     c = (h * len(rows) + r - rows.start) * P
-                    nc.tensor.transpose(x_bank[s, rows.start][:, c : c + P], x_sb[s, r][:, h : 2 * P : 2], ident[:])
+                    nc.tensor.transpose(x_bank[s, rows.start][:, c : c + P], x_pairs[s, r][:, h : 2 * P : 2], ident[:])
 
-        def group_x(s, rows=range(ROWS)):
+        def group_x(s, rows=BOTH):
             if s not in x_grouped:
-                x_grouped[s] = ring("xg", s, 4, [P, ROWS * P * PACK], BF16)
+                x_grouped[s] = ring("xg", s, 4, [P, STEP_USERS * PACK], BF16)
+            pairs = x_grouped[s][:].bitcast(F32)[:, 2 * P * rows.start : 2 * P * rows.stop]
             nc.scalar.copy(
-                out=x_grouped[s][:].bitcast(F32)[:, 2 * P * rows.start : 2 * P * rows.stop].rearrange("p (c h) -> p c h", h=2),
+                out=pairs.rearrange("p (c h) -> p c h", h=2),
                 in_=x_bank[s, rows.start][:, : 2 * len(rows) * P].rearrange("p (h c) -> p c h", h=2),
             )
 
-        def quantize_x(s, rows=range(ROWS)):
+        def quantize_x(s, rows=BOTH):
             if s not in x_codes:
-                x_codes[s] = ring("xc", s, 3, [P, ROWS * P], U32)
-                x_plane[s] = ring("xs", s, 3, [P, ROWS * P], U8)
+                x_codes[s] = ring("xc", s, 3, [P, STEP_USERS], U32)
+                x_plane[s] = ring("xs", s, 3, [P, STEP_USERS], U8)
             cols = slice(rows.start * P, rows.stop * P)
             nc.vector.quantize_mx(
                 out=x_codes[s][:, cols].bitcast(FP8X4),
@@ -152,94 +157,97 @@ def tile_implicit_als_gradient_s14_kernel(tc, x, yt_words, yt_scales, pref, conf
             )
 
         def scale_x(s):
-            market, first, rows = steps[s]
-            rx_t[s] = ring("rxt", s, 2, [P, PACK, rows * P], F32)
-            slots = x_grouped[s][:].rearrange("p (c t) -> p t c", t=PACK)
+            rx_t[s] = ring("rxt", s, 2, [P, PACK, STEP_USERS], F32)
+            by_t = x_grouped[s][:].rearrange("p (c t) -> p t c", t=PACK)
             for t in range(PACK):
-                nc.scalar.activation(out=rx_t[s][:, t, :], in_=slots[:, t, :], func=ACT.Copy, scale=ridge_col[:, market, t : t + 1])
+                nc.scalar.activation(out=rx_t[s][:, t, :], in_=by_t[:, t, :], func=ACT.Copy, scale=ridge_col[:, market_of(s), t : t + 1])
 
-        def transpose_rx(s):
-            for r in range(steps[s][2]):
+        def ridge_term(s):
+            for r in BOTH:
                 rx_bank[s, r] = next_bank()
                 for t in range(PACK):
                     nc.tensor.transpose(rx_bank[s, r][:, t * P : (t + 1) * P], rx_t[s][:, t, r * P : (r + 1) * P], ident[:])
-
-        def copy_rx(s):
-            rows = steps[s][2]
-            result[s] = ring("res", s, 6, [P, rows, FACTORS], F32)
-            for r in range(rows):
+            result[s] = ring("res", s, RESULTS, [P, ROWS, FACTORS], F32)
+            for r in BOTH:
                 nc.scalar.copy(
                     out=result[s][:, r, :].rearrange("u (p t) -> u p t", t=PACK),
                     in_=rx_bank[s, r][:].rearrange("u (t p) -> u p t", t=PACK),
                 )
 
-        def scores(s, rows=range(ROWS)):
-            market = steps[s][0]
+
+        def scores(s, rows=BOTH):
+            market = market_of(s)
             for r in rows:
-                for n in range(ITEMS // BANK):
-                    score_bank[s, r, n] = next_bank()
+                for g in range(ITEM_PASSES):
+                    score_bank[s, r, g] = next_bank()
                     nc.tensor.matmul_mx(
-                        out=score_bank[s, r, n][:],
+                        out=score_bank[s, r, g][:],
                         lhsT=x_codes[s][:, r * P : (r + 1) * P].bitcast(FP8X4),
                         lhsT_scale=x_plane[s][:, r * P : (r + 1) * P],
-                        rhs=yt_sb[market][:, 2 * n * BANK : 2 * (n + 1) * BANK].bitcast(FP4X4),
-                        rhs_scale=yt_plane[:, market, n * BANK : (n + 1) * BANK],
+                        rhs=yt_sb[market][:, 2 * g * BANK : 2 * (g + 1) * BANK].bitcast(FP4X4),
+                        rhs_scale=yt_plane[:, market, g * BANK : (g + 1) * BANK],
                         start=True,
                         stop=True,
                     )
 
-        def subtract_pref(s, banks):
-            rows = steps[s][2]
-            if s not in resid:
-                resid[s] = ring("resid", s, 2, [P, rows * ITEMS], F32)
-            for b in banks:
-                for r, n in [divmod(b, ITEM_PASSES)]:
-                    q = (r * ITEM_PASSES + n) * P
-                    nc.vector.tensor_tensor(
-                        out=resid[s][:].rearrange("u (h q e) -> u h q e", h=2, e=2)[:, :, q : q + P, :],
-                        in0=score_bank[s, r, n][:].rearrange("u (q h e) -> u h q e", h=2, e=2),
-                        in1=pref_sb[s, r][:, n * BANK : (n + 1) * BANK].rearrange("u (q h e) -> u h q e", h=2, e=2),
-                        op=ALU.subtract,
-                    )
+        def by_pair(ap):
+            return ap.rearrange("u (h q j) -> u h q j", h=2, j=2)
 
-        def weigh(engine, s, cols):
-            quads = slice(cols.start // PACK, cols.stop // PACK)
+        def subtract_pref(s, banks):
+            if s not in resid:
+                resid[s] = ring("resid", s, 2, [P, E_COLS], F32)
+            for b in banks:
+                r, g = divmod(b, ITEM_PASSES)
+                nc.vector.tensor_tensor(
+                    out=by_pair(resid[s][:])[:, :, b * P : (b + 1) * P, :],
+                    in0=score_bank[s, r, g][:].rearrange("u (q h j) -> u h q j", h=2, j=2),
+                    in1=pref_sb[s, r][:, g * BANK : (g + 1) * BANK].rearrange("u (q h j) -> u h q j", h=2, j=2),
+                    op=ALU.subtract,
+                )
+
+        def weigh(engine, s, quads):
             engine.tensor_tensor(
-                out=e_sb[s][:].rearrange("u (h q e) -> u h q e", h=2, e=2)[:, :, quads, :],
-                in0=resid[s][:].rearrange("u (h q e) -> u h q e", h=2, e=2)[:, :, quads, :],
-                in1=conf_sb[s][:].rearrange("u r (q h e) -> u h (r q) e", h=2, e=2)[:, :, quads, :],
+                out=by_pair(e_sb[s][:])[:, :, quads, :],
+                in0=by_pair(resid[s][:])[:, :, quads, :],
+                in1=conf_sb[s][:].rearrange("u r (q h j) -> u h (r q) j", h=2, j=2)[:, :, quads, :],
                 op=ALU.mult,
             )
 
-        def transpose_e(s):
-            words = e_sb[s][:].bitcast(F32).rearrange("u (h q) -> u h q", h=2)
-            for r in range(steps[s][2]):
+        def new_e(s):
+            e_sb[s] = ring("e", s, 2, [P, E_COLS], BF16)
+
+        def weigh_on_pool(s, banks_read):
+            split = (E_COLS - (banks_read * POOL_COLS_PER_BANK - POOL_COLS_LESS)) // PACK
+            new_e(s)
+            weigh(nc.gpsimd, s, slice(split, E_COLS // PACK))
+            return slice(0, split)
+
+        def turn_e(s):
+            pairs = e_sb[s][:].bitcast(F32).rearrange("u (h q) -> u h q", h=2)
+            for r in BOTH:
                 e_bank[s, r] = next_bank()
                 for g in range(ITEM_PASSES):
                     for h in range(2):
                         c = (2 * g + h) * P
                         q = (r * ITEM_PASSES + g) * P
-                        nc.tensor.transpose(e_bank[s, r][:, c : c + P], words[:, h, q : q + P], ident[:])
-
-        def group_e(s):
-            rows = steps[s][2]
-            e_grouped[s] = ring("e", s, 2, [P, rows * ITEMS], BF16)
-            words = e_grouped[s][:].bitcast(F32)
-            for r in range(rows):
+                        nc.tensor.transpose(e_bank[s, r][:, c : c + P], pairs[:, h, q : q + P], ident[:])
+            e_grouped[s] = ring("e", s, 2, [P, E_COLS], BF16)
+            grouped_pairs = e_grouped[s][:].bitcast(F32)
+            for r in BOTH:
                 nc.scalar.copy(
-                    out=words[:, r * BANK : (r + 1) * BANK].rearrange("p (g u h) -> p g u h", g=ITEM_PASSES, h=2),
+                    out=grouped_pairs[:, r * BANK : (r + 1) * BANK].rearrange("p (g u h) -> p g u h", g=ITEM_PASSES, h=2),
                     in_=e_bank[s, r][:].rearrange("p (g h u) -> p g u h", g=ITEM_PASSES, h=2),
                 )
 
         def quantize_e(s):
-            rows = steps[s][2]
-            e_codes[s] = ring("ec", s, 2, [P, rows * ITEM_PASSES * P], U32)
-            e_plane[s] = ring("es", s, 2, [P, rows * ITEM_PASSES * P], U8)
+            e_codes[s] = ring("ec", s, 2, [P, E_COLS // PACK], U32)
+            e_plane[s] = ring("es", s, 2, [P, E_COLS // PACK], U8)
             nc.vector.quantize_mx(out=e_codes[s][:].bitcast(FP8X4), scales=e_plane[s][:], in_=e_grouped[s][:])
 
+
         def gradient(s):
-            market, first, rows = steps[s]
-            for r in range(rows):
+            market = market_of(s)
+            for r in BOTH:
                 grad_bank[s, r] = next_bank()
                 for g in range(ITEM_PASSES):
                     c = (r * ITEM_PASSES + g) * P
@@ -254,46 +262,22 @@ def tile_implicit_als_gradient_s14_kernel(tc, x, yt_words, yt_scales, pref, conf
                     )
 
         def finish(s):
-            last = s >= n_steps - 2
-            for r in range(steps[s][2]):
+            row_by_row = s >= STEPS - 2
+            for r in BOTH:
                 nc.vector.tensor_tensor(out=result[s][:, r, :], in0=grad_bank[s, r][:], in1=result[s][:, r, :], op=ALU.add)
-                if last:
+                if row_by_row:
                     nc.sync.dma_start(out=users_of(out, s)[:, r, :], in_=result[s][:, r, :])
-            if not last:
+            if not row_by_row:
                 nc.sync.dma_start(out=users_of(out, s), in_=result[s][:])
 
-        def live(s):
-            return 0 <= s < n_steps
-
-        def pool_share(s, banks_read):
-            width = steps[s][2] * ITEMS
-            share = min(width, max(0, banks_read * POOL_COLS_PER_BANK - POOL_COLS_LESS))
-            e_sb[s] = ring("e", s, 2, [P, width], BF16)
-            if share > 0:
-                weigh(nc.gpsimd, s, slice(width - share, width))
-            return slice(0, width - share)
-
-        def warm(passes):
-            s = n_steps - 1
-            for n in range(passes):
-                bank = next_bank()
-                nc.tensor.matmul_mx(
-                    out=bank[:],
-                    lhsT=x_codes[s][:, :P].bitcast(FP8X4),
-                    lhsT_scale=x_plane[s][:, :P],
-                    rhs=yt_sb[MARKETS - 1][:, : 2 * BANK].bitcast(FP4X4),
-                    rhs_scale=yt_plane[:, MARKETS - 1, :BANK],
-                    start=True,
-                    stop=True,
-                )
-
-        load_x(0, range(0, 1))
+        first_row, second_row = range(0, 1), range(1, 2)
+        load_x(0, first_row)
         load_yt(0)
-        load_x(0, range(1, 2))
+        load_x(0, second_row)
         load_plane(yt_plane, yt_scales, slice(0, 1))
         load_x(1)
-        load_pref(0, range(0, 1))
-        load_pref(0, range(1, 2))
+        load_pref(0, first_row)
+        load_pref(0, second_row)
         load_x(2)
         load_pref(1)
         load_conf(0)
@@ -301,52 +285,54 @@ def tile_implicit_als_gradient_s14_kernel(tc, x, yt_words, yt_scales, pref, conf
         load_x(3)
         load_for(2)
         load_plane(yt_plane, yt_scales, slice(1, 2))
+        load_pref(3)
+        load_conf(2)
+        load_y(0)
         load_plane(y_plane, y_scales, slice(0, ITEM_PASSES))
-        for k in range(3, LOAD_AHEAD + 2):
+        load_x(5)
+        for k in range(4, 2 + LOAD_AHEAD):
             load_for(k)
             if k == LATE_PLANES:
                 load_plane(yt_plane, yt_scales, slice(2, MARKETS))
                 load_plane(y_plane, y_scales, slice(ITEM_PASSES, MARKETS * ITEM_PASSES))
 
-        for r in range(ROWS):
-            transpose_x(0, range(r, r + 1))
-            group_x(0, range(r, r + 1))
-            quantize_x(0, range(r, r + 1))
-        scores(0, range(0, 1))
+        for rows in (first_row, second_row):
+            transpose_x(0, rows)
+            group_x(0, rows)
+            quantize_x(0, rows)
+        scores(0, first_row)
         transpose_x(1)
         group_x(1)
-        scores(0, range(1, 2))
-        subtract_pref(0, [0, 1])
+        scores(0, second_row)
+        subtract_pref(0, range(0, ITEM_PASSES))
         quantize_x(1)
         scores(1)
-        subtract_pref(0, [2, 3])
+        subtract_pref(0, range(ITEM_PASSES, SCORE_BANKS))
         transpose_x(2)
         group_x(2)
         transpose_x(3)
         group_x(3)
         nc.scalar.copy(out=ridge_col[:], in_=ridge_bf[:])
         scale_x(0)
-        rest = pool_share(0, HEAD0)
-        subtract_pref(1, [0, 1, 2])
+        rest = weigh_on_pool(0, SCORE_BANKS - 1)
+        subtract_pref(1, range(0, SCORE_BANKS - 1))
         quantize_x(2)
         scores(2)
         weigh(nc.vector, 0, rest)
         quantize_x(3)
-        subtract_pref(1, [3])
+        subtract_pref(1, range(SCORE_BANKS - 1, SCORE_BANKS))
         scale_x(1)
-        transpose_rx(0)
-        copy_rx(0)
+        ridge_term(0)
 
-        for k in range(2, n_steps):
+        for k in range(2, STEPS):
             load_for(k + LOAD_AHEAD)
             if live(k - 3):
                 gradient(k - 3)
-            rest = pool_share(k - 1, 2 * steps[k][2] + (steps[k - 3][2] if live(k - 3) else 0))
-            subtract_pref(k, range(2 * steps[k][2]))
+            rest = weigh_on_pool(k - 1, SCORE_BANKS + (ROWS if live(k - 3) else 0))
+            subtract_pref(k, range(SCORE_BANKS))
             if live(k - 3):
                 finish(k - 3)
-            transpose_e(k - 2)
-            group_e(k - 2)
+            turn_e(k - 2)
             if live(k + 2):
                 transpose_x(k + 2)
                 group_x(k + 2)
@@ -358,31 +344,22 @@ def tile_implicit_als_gradient_s14_kernel(tc, x, yt_words, yt_scales, pref, conf
                 quantize_x(k + 2)
             if live(k + 1):
                 scores(k + 1)
-            else:
-                warm(WARM[0])
-            transpose_rx(k - 1)
-            copy_rx(k - 1)
-            if k == n_steps - 2:
+            ridge_term(k - 1)
+            if k == STEPS - 2:
                 scale_x(k + 1)
-            if k == n_steps - 1:
-                transpose_rx(k)
-                copy_rx(k)
+            if k == STEPS - 1:
+                ridge_term(k)
 
-        a, b, c = n_steps - 3, n_steps - 2, n_steps - 1
-        warm(WARM[1])
-        transpose_e(b)
-        group_e(b)
-        gradient(a)
-        warm(WARM[2])
-        rest = pool_share(c, 0)
-        weigh(nc.vector, c, rest)
-        quantize_e(b)
-        finish(a)
-        transpose_e(c)
-        group_e(c)
-        gradient(b)
-        warm(WARM[3])
-        quantize_e(c)
-        finish(b)
-        gradient(c)
-        finish(c)
+        last = STEPS - 1
+        turn_e(last - 1)
+        gradient(last - 2)
+        new_e(last)
+        weigh(nc.vector, last, slice(0, E_COLS // PACK))
+        quantize_e(last - 1)
+        finish(last - 2)
+        turn_e(last)
+        gradient(last - 1)
+        quantize_e(last)
+        finish(last - 1)
+        gradient(last)
+        finish(last)

from contextlib import ExitStack

import concourse.mybir as mybir
from concourse.masks import make_identity

MARKETS, USERS, FACTORS, ITEMS = 4, 768, 512, 1024
FLOPS = 2 * 2 * MARKETS * USERS * FACTORS * ITEMS

F32 = mybir.dt.float32
BF16 = mybir.dt.bfloat16
I32 = mybir.dt.int32
U32 = mybir.dt.uint32
U8 = mybir.dt.uint8
FP8X4 = mybir.dt.float8_e4m3fn_x4
FP4X4 = mybir.dt.float4_e2m1fn_x4
ALU = mybir.AluOpType
ACT = mybir.ActivationFunctionType

P = 128
PACK = 4
BANK = 512
BANKS = 8
QUADRANTS = 4
ITEM_PASSES = ITEMS // (P * PACK)
ROWS = 2
BOTH = range(ROWS)
STEP_USERS = ROWS * P
STEPS_PER_MARKET = USERS // STEP_USERS
STEPS = MARKETS * STEPS_PER_MARKET
SCORE_BANKS = ROWS * ITEM_PASSES
E_COLS = ROWS * ITEMS

POOL_COLS_PER_BANK = 256
POOL_COLS_LESS = 192
LOAD_AHEAD = 5
RESULTS = 8
LATE_PLANES = 5


def tile_implicit_als_gradient_s14_kernel(tc, x, yt_words, yt_scales, pref, conf, y_words, y_scales, ridge, out):
    nc = tc.nc

    def live(s):
        return 0 <= s < STEPS

    def market_of(s):
        return s // STEPS_PER_MARKET

    def opens_market(s):
        return live(s) and s % STEPS_PER_MARKET == 0

    def users_of(ap, s):
        first = s % STEPS_PER_MARKET * STEP_USERS
        return ap[market_of(s), first : first + STEP_USERS, :].rearrange("(p r) c -> p r c", r=ROWS)

    with ExitStack() as ctx:
        keep = ctx.enter_context(tc.tile_pool(name="keep", bufs=1))
        work = ctx.enter_context(tc.tile_pool(name="work", bufs=1))
        psum = ctx.enter_context(tc.psum_pool(name="psum", bufs=1))
        ctx.enter_context(tc.manual_schedule())

        banks_taken = []

        def next_bank():
            n = len(banks_taken)
            banks_taken.append(n)
            return psum.tile([P, BANK], F32, name="bank%d" % n, tag="bank%d" % (n % BANKS))

        def ring(kind, s, depth, shape, dtype):
            return work.tile(shape, dtype, name="%s%d" % (kind, s), tag="%s%d" % (kind, s % depth), align_bytes=64)

        ident = keep.tile([P, P], F32)
        yt_plane = keep.tile([P, MARKETS, ITEMS], U8, align_bytes=64)
        y_plane = keep.tile([P, MARKETS * ITEM_PASSES, FACTORS], U8, align_bytes=64)
        ridge_bf = keep.tile([P, MARKETS, PACK], BF16)
        ridge_col = keep.tile([P, MARKETS, PACK], F32)

        nc.vector.memset(yt_plane[:].rearrange("p m n -> p (m n)").bitcast(I32), 0)
        nc.vector.memset(y_plane[:].rearrange("p m n -> p (m n)").bitcast(I32), 0)
        make_identity(nc, ident[:])

        x_pairs, pref_sb, conf_sb, yt_sb, y_sb = {}, {}, {}, {}, {}
        x_bank, x_grouped, x_codes, x_plane, rx_t, rx_bank, result = {}, {}, {}, {}, {}, {}, {}
        score_bank, resid, e_sb, e_bank, e_grouped, e_codes, e_plane, grad_bank = {}, {}, {}, {}, {}, {}, {}, {}


        def load_plane(plane, scales, passes):
            for q in range(QUADRANTS):
                nc.sync.dma_start(
                    out=plane[32 * q : 32 * q + 4, passes, :].bitcast(I32),
                    in_=scales[passes, 4 * q : 4 * q + 4, :].rearrange("g r n -> r g n").bitcast(I32),
                )

        def load_x(s, rows=BOTH):
            tile = keep.tile([P, len(rows), FACTORS], BF16, name="x%d_%d" % (s, rows.start))
            nc.sync.dma_start(out=tile[:], in_=users_of(x, s)[:, rows.start : rows.stop, :])
            for r in rows:
                x_pairs[s, r] = tile[:].bitcast(F32)[:, r - rows.start, :]

        def load_pref(s, rows=BOTH):
            tile = keep.tile([P, len(rows), ITEMS], BF16, name="pref%d_%d" % (s, rows.start))
            nc.sync.dma_start(out=tile[:], in_=users_of(pref, s)[:, rows.start : rows.stop, :])
            for r in rows:
                pref_sb[s, r] = tile[:, r - rows.start, :]

        def load_conf(s):
            conf_sb[s] = keep.tile([P, ROWS, ITEMS], BF16, name="conf%d" % s)
            nc.sync.dma_start(out=conf_sb[s][:], in_=users_of(conf, s))

        def load_yt(market):
            yt_sb[market] = keep.tile([P, 2 * ITEMS], U8, name="yt%d" % market, align_bytes=64)
            nc.sync.dma_start(out=yt_sb[market][:].bitcast(I32), in_=yt_words[market].bitcast(I32))

        def load_y(market):
            y_sb[market] = keep.tile([P, ITEM_PASSES, 2 * FACTORS], U8, name="y%d" % market, align_bytes=64)
            passes = y_words[ITEM_PASSES * market : ITEM_PASSES * (market + 1)]
            nc.sync.dma_start(out=y_sb[market][:].bitcast(I32), in_=passes.rearrange("g p n -> p g n").bitcast(I32))

        def load_for(k):
            if live(k):
                load_pref(k)
            if live(k - 1):
                load_conf(k - 1)
            if opens_market(k - 3):
                load_y(market_of(k - 3))
            if live(k + 2):
                load_x(k + 2)
            if opens_market(k + 1):
                load_yt(market_of(k + 1))


        def transpose_x(s, rows=BOTH):
            x_bank[s, rows.start] = next_bank()
            for h in range(2):
                for r in rows:
                    c = (h * len(rows) + r - rows.start) * P
                    nc.tensor.transpose(x_bank[s, rows.start][:, c : c + P], x_pairs[s, r][:, h : 2 * P : 2], ident[:])

        def group_x(s, rows=BOTH):
            if s not in x_grouped:
                x_grouped[s] = ring("xg", s, 4, [P, STEP_USERS * PACK], BF16)
            pairs = x_grouped[s][:].bitcast(F32)[:, 2 * P * rows.start : 2 * P * rows.stop]
            nc.scalar.copy(
                out=pairs.rearrange("p (c h) -> p c h", h=2),
                in_=x_bank[s, rows.start][:, : 2 * len(rows) * P].rearrange("p (h c) -> p c h", h=2),
            )

        def quantize_x(s, rows=BOTH):
            if s not in x_codes:
                x_codes[s] = ring("xc", s, 3, [P, STEP_USERS], U32)
                x_plane[s] = ring("xs", s, 3, [P, STEP_USERS], U8)
            cols = slice(rows.start * P, rows.stop * P)
            nc.vector.quantize_mx(
                out=x_codes[s][:, cols].bitcast(FP8X4),
                scales=x_plane[s][:, cols],
                in_=x_grouped[s][:, PACK * cols.start : PACK * cols.stop],
            )

        def scale_x(s):
            rx_t[s] = ring("rxt", s, 2, [P, PACK, STEP_USERS], F32)
            by_t = x_grouped[s][:].rearrange("p (c t) -> p t c", t=PACK)
            for t in range(PACK):
                nc.scalar.activation(out=rx_t[s][:, t, :], in_=by_t[:, t, :], func=ACT.Copy, scale=ridge_col[:, market_of(s), t : t + 1])

        def ridge_term(s):
            for r in BOTH:
                rx_bank[s, r] = next_bank()
                for t in range(PACK):
                    nc.tensor.transpose(rx_bank[s, r][:, t * P : (t + 1) * P], rx_t[s][:, t, r * P : (r + 1) * P], ident[:])
            result[s] = ring("res", s, RESULTS, [P, ROWS, FACTORS], F32)
            for r in BOTH:
                nc.scalar.copy(
                    out=result[s][:, r, :].rearrange("u (p t) -> u p t", t=PACK),
                    in_=rx_bank[s, r][:].rearrange("u (t p) -> u p t", t=PACK),
                )


        def scores(s, rows=BOTH):
            market = market_of(s)
            for r in rows:
                for g in range(ITEM_PASSES):
                    score_bank[s, r, g] = next_bank()
                    nc.tensor.matmul_mx(
                        out=score_bank[s, r, g][:],
                        lhsT=x_codes[s][:, r * P : (r + 1) * P].bitcast(FP8X4),
                        lhsT_scale=x_plane[s][:, r * P : (r + 1) * P],
                        rhs=yt_sb[market][:, 2 * g * BANK : 2 * (g + 1) * BANK].bitcast(FP4X4),
                        rhs_scale=yt_plane[:, market, g * BANK : (g + 1) * BANK],
                        start=True,
                        stop=True,
                    )

        def by_pair(ap):
            return ap.rearrange("u (h q j) -> u h q j", h=2, j=2)

        def subtract_pref(s, banks):
            if s not in resid:
                resid[s] = ring("resid", s, 2, [P, E_COLS], F32)
            for b in banks:
                r, g = divmod(b, ITEM_PASSES)
                nc.vector.tensor_tensor(
                    out=by_pair(resid[s][:])[:, :, b * P : (b + 1) * P, :],
                    in0=score_bank[s, r, g][:].rearrange("u (q h j) -> u h q j", h=2, j=2),
                    in1=pref_sb[s, r][:, g * BANK : (g + 1) * BANK].rearrange("u (q h j) -> u h q j", h=2, j=2),
                    op=ALU.subtract,
                )

        def weigh(engine, s, quads):
            engine.tensor_tensor(
                out=by_pair(e_sb[s][:])[:, :, quads, :],
                in0=by_pair(resid[s][:])[:, :, quads, :],
                in1=conf_sb[s][:].rearrange("u r (q h j) -> u h (r q) j", h=2, j=2)[:, :, quads, :],
                op=ALU.mult,
            )

        def new_e(s):
            e_sb[s] = ring("e", s, 2, [P, E_COLS], BF16)

        def weigh_on_pool(s, banks_read):
            split = (E_COLS - (banks_read * POOL_COLS_PER_BANK - POOL_COLS_LESS)) // PACK
            new_e(s)
            weigh(nc.gpsimd, s, slice(split, E_COLS // PACK))
            return slice(0, split)

        def turn_e(s):
            pairs = e_sb[s][:].bitcast(F32).rearrange("u (h q) -> u h q", h=2)
            for r in BOTH:
                e_bank[s, r] = next_bank()
                for g in range(ITEM_PASSES):
                    for h in range(2):
                        c = (2 * g + h) * P
                        q = (r * ITEM_PASSES + g) * P
                        nc.tensor.transpose(e_bank[s, r][:, c : c + P], pairs[:, h, q : q + P], ident[:])
            e_grouped[s] = ring("e", s, 2, [P, E_COLS], BF16)
            grouped_pairs = e_grouped[s][:].bitcast(F32)
            for r in BOTH:
                nc.scalar.copy(
                    out=grouped_pairs[:, r * BANK : (r + 1) * BANK].rearrange("p (g u h) -> p g u h", g=ITEM_PASSES, h=2),
                    in_=e_bank[s, r][:].rearrange("p (g h u) -> p g u h", g=ITEM_PASSES, h=2),
                )

        def quantize_e(s):
            e_codes[s] = ring("ec", s, 2, [P, E_COLS // PACK], U32)
            e_plane[s] = ring("es", s, 2, [P, E_COLS // PACK], U8)
            nc.vector.quantize_mx(out=e_codes[s][:].bitcast(FP8X4), scales=e_plane[s][:], in_=e_grouped[s][:])


        def gradient(s):
            market = market_of(s)
            for r in BOTH:
                grad_bank[s, r] = next_bank()
                for g in range(ITEM_PASSES):
                    c = (r * ITEM_PASSES + g) * P
                    nc.tensor.matmul_mx(
                        out=grad_bank[s, r][:],
                        lhsT=e_codes[s][:, c : c + P].bitcast(FP8X4),
                        lhsT_scale=e_plane[s][:, c : c + P],
                        rhs=y_sb[market][:, g, :].bitcast(FP4X4),
                        rhs_scale=y_plane[:, market * ITEM_PASSES + g, :],
                        start=(g == 0),
                        stop=(g == ITEM_PASSES - 1),
                    )

        def finish(s):
            row_by_row = s >= STEPS - 2
            for r in BOTH:
                nc.vector.tensor_tensor(out=result[s][:, r, :], in0=grad_bank[s, r][:], in1=result[s][:, r, :], op=ALU.add)
                if row_by_row:
                    nc.sync.dma_start(out=users_of(out, s)[:, r, :], in_=result[s][:, r, :])
            if not row_by_row:
                nc.sync.dma_start(out=users_of(out, s), in_=result[s][:])

        first_row, second_row = range(0, 1), range(1, 2)
        load_x(0, first_row)
        load_yt(0)
        load_x(0, second_row)
        load_plane(yt_plane, yt_scales, slice(0, 1))
        load_x(1)
        load_pref(0, first_row)
        load_pref(0, second_row)
        load_x(2)
        load_pref(1)
        load_conf(0)
        nc.sync.dma_start(out=ridge_bf[:], in_=ridge.rearrange("m (p t) -> p m t", t=PACK))
        load_x(3)
        load_for(2)
        load_plane(yt_plane, yt_scales, slice(1, 2))
        load_pref(3)
        load_conf(2)
        load_y(0)
        load_plane(y_plane, y_scales, slice(0, ITEM_PASSES))
        load_x(5)
        for k in range(4, 2 + LOAD_AHEAD):
            load_for(k)
            if k == LATE_PLANES:
                load_plane(yt_plane, yt_scales, slice(2, MARKETS))
                load_plane(y_plane, y_scales, slice(ITEM_PASSES, MARKETS * ITEM_PASSES))

        for rows in (first_row, second_row):
            transpose_x(0, rows)
            group_x(0, rows)
            quantize_x(0, rows)
        scores(0, first_row)
        transpose_x(1)
        group_x(1)
        scores(0, second_row)
        subtract_pref(0, range(0, ITEM_PASSES))
        quantize_x(1)
        scores(1)
        subtract_pref(0, range(ITEM_PASSES, SCORE_BANKS))
        transpose_x(2)
        group_x(2)
        transpose_x(3)
        group_x(3)
        nc.scalar.copy(out=ridge_col[:], in_=ridge_bf[:])
        scale_x(0)
        rest = weigh_on_pool(0, SCORE_BANKS - 1)
        subtract_pref(1, range(0, SCORE_BANKS - 1))
        quantize_x(2)
        scores(2)
        weigh(nc.vector, 0, rest)
        quantize_x(3)
        subtract_pref(1, range(SCORE_BANKS - 1, SCORE_BANKS))
        scale_x(1)
        ridge_term(0)

        for k in range(2, STEPS):
            load_for(k + LOAD_AHEAD)
            if live(k - 3):
                gradient(k - 3)
            rest = weigh_on_pool(k - 1, SCORE_BANKS + (ROWS if live(k - 3) else 0))
            subtract_pref(k, range(SCORE_BANKS))
            if live(k - 3):
                finish(k - 3)
            turn_e(k - 2)
            if live(k + 2):
                transpose_x(k + 2)
                group_x(k + 2)
            if live(k + 1):
                scale_x(k)
            weigh(nc.vector, k - 1, rest)
            quantize_e(k - 2)
            if live(k + 2):
                quantize_x(k + 2)
            if live(k + 1):
                scores(k + 1)
            ridge_term(k - 1)
            if k == STEPS - 2:
                scale_x(k + 1)
            if k == STEPS - 1:
                ridge_term(k)

        last = STEPS - 1
        turn_e(last - 1)
        gradient(last - 2)
        new_e(last)
        weigh(nc.vector, last, slice(0, E_COLS // PACK))
        quantize_e(last - 1)
        finish(last - 2)
        turn_e(last)
        gradient(last - 1)
        quantize_e(last)
        finish(last - 1)
        gradient(last)
        finish(last)
